import numpy as np
import ml_dtypes

BF16 = ml_dtypes.bfloat16


def bf(x):
    return np.asarray(x, np.float32).astype(BF16)


def f32(x):
    return np.asarray(x, np.float32)


def f64(x):
    return np.asarray(x).astype(np.float64)


def striped(idx):
    return np.concatenate([l.reshape(-1, 16).T for l in idx])


def rows(idx, k):
    return np.tile(np.repeat(idx, 16, axis=0), (k // (16 * 8), 1))


def look(tab, idx):
    return np.take_along_axis(f64(tab), rows(idx, len(tab)), axis=1)


K, S, D, V, N = 128, 2048, 3, 512, 1536


def setup_inputs():
    return {"tab": f32(np.random.standard_normal((K, S))), "x0": f32(np.random.standard_normal((K, V))), "offs": striped(np.stack([np.random.permutation(S)[:N] for _ in range(8)]))}


def reference(tab, x0, offs):
    idx = np.stack([g.T.reshape(-1) for g in np.split(offs, 8)])
    x = f64(x0)
    for d in range(D):
        x = np.minimum(x, look(tab, idx[:, d * V:(d + 1) * V]))
    return x

@@ -1,0 +1,23 @@
+import concourse.mybir as mybir
+
+F32, U16 = mybir.dt.float32, mybir.dt.uint16
+MIN = mybir.AluOpType.min
+ROWS, TABLE_COLS, D, V = 128, 2048, 3, 512
+LIST_COLS = V // 16
+
+def tile_lookup_pool_min_out_kernel(tc, tab, x0, offs, out):
+    nc = tc.nc
+    with tc.tile_pool(name="held", bufs=1) as held:
+        offsets = held.tile([ROWS, D * LIST_COLS], U16, name="offsets")
+        table = held.tile([ROWS, TABLE_COLS], F32, name="table")
+        x = [held.tile([ROWS, V], F32, name=f"x{d}") for d in range(D + 1)]
+
+        nc.sync.dma_start(offsets[:], offs)
+        nc.scalar.dma_start(table[:], tab)
+        nc.sync.dma_start(x[0][:], x0)
+
+        for d in range(D):
+            piece = offsets[:, d * LIST_COLS : (d + 1) * LIST_COLS]
+            nc.vector.tensor_tensor(x[d + 1][:], table[:].indirect(piece), x[d][:], MIN)
+
+        nc.sync.dma_start(out, x[D][:])

@@ -12,9 +12,11 @@ def tile_lookup_pool_min_out_kernel(tc, tab, x0, offs, out):
         table = held.tile([ROWS, TABLE_COLS], F32, name="table")
         x = [held.tile([ROWS, V], F32, name=f"x{d}") for d in range(D + 1)]
 
+        half = TABLE_COLS // 2
         nc.sync.dma_start(offsets[:], offs)
-        nc.scalar.dma_start(table[:], tab)
-        nc.sync.dma_start(x[0][:], x0)
+        nc.scalar.dma_start(table[:, :half], tab[:, :half])
+        nc.sync.dma_start(table[:, half:], tab[:, half:])
+        nc.scalar.dma_start(x[0][:], x0)
 
         for d in range(D):
             piece = offsets[:, d * LIST_COLS : (d + 1) * LIST_COLS]

@@ -12,10 +12,8 @@ def tile_lookup_pool_min_out_kernel(tc, tab, x0, offs, out):
         table = held.tile([ROWS, TABLE_COLS], F32, name="table")
         x = [held.tile([ROWS, V], F32, name=f"x{d}") for d in range(D + 1)]
 
-        half = TABLE_COLS // 2
+        nc.sync.dma_start(table[:], tab)
         nc.sync.dma_start(offsets[:], offs)
-        nc.scalar.dma_start(table[:, :half], tab[:, :half])
-        nc.sync.dma_start(table[:, half:], tab[:, half:])
         nc.scalar.dma_start(x[0][:], x0)
 
         for d in range(D):

import concourse.mybir as mybir

F32, U16 = mybir.dt.float32, mybir.dt.uint16
MIN = mybir.AluOpType.min
ROWS, TABLE_COLS, D, V = 128, 2048, 3, 512
LIST_COLS = V // 16

def tile_lookup_pool_min_out_kernel(tc, tab, x0, offs, out):
    nc = tc.nc
    with tc.tile_pool(name="held", bufs=1) as held:
        offsets = held.tile([ROWS, D * LIST_COLS], U16, name="offsets")
        table = held.tile([ROWS, TABLE_COLS], F32, name="table")
        x = [held.tile([ROWS, V], F32, name=f"x{d}") for d in range(D + 1)]

        nc.sync.dma_start(table[:], tab)
        nc.sync.dma_start(offsets[:], offs)
        nc.scalar.dma_start(x[0][:], x0)

        for d in range(D):
            piece = offsets[:, d * LIST_COLS : (d + 1) * LIST_COLS]
            nc.vector.tensor_tensor(x[d + 1][:], table[:].indirect(piece), x[d][:], MIN)

        nc.sync.dma_start(out, x[D][:])
